import numpy as np
import ml_dtypes


def mxq(x, axis, fmt="e4m3"):
    dtype, down = {"e4m3": (ml_dtypes.float8_e4m3fn, 7), "e5m2": (ml_dtypes.float8_e5m2, 14)}[fmt]
    v = np.moveaxis(np.asarray(x, np.float32).astype(ml_dtypes.bfloat16).astype(np.float64), axis, -1)
    blocks = v.reshape(v.shape[:-1] + (-1, 32))
    amax = np.abs(blocks).max(-1, keepdims=True)
    byte = np.maximum(np.where(amax > 0, np.frexp(amax)[1] - 1 + 127, 0) - down, 1)
    scale = np.exp2(byte - 127.0)
    codes = (blocks / scale).astype(np.float32).astype(dtype).astype(np.float64)
    return np.moveaxis((codes * scale).reshape(v.shape), -1, axis)


WIDE = False


def mx_kscale(k):
    if not WIDE:
        return np.ones(k)
    levels = np.array([10, -10, 5, -5, 0])
    if k % 512:
        return np.exp2(np.random.permutation(np.resize(levels, k // 32))).repeat(32)
    a = np.empty((k // 512, 16))
    for p in range(k // 512):
        a[p, :8] = np.random.permutation(np.resize(levels, 8))
        for g in range(8):
            far = levels[np.abs(levels - a[p, g]) >= 10]
            a[p, g + 8] = far[np.random.randint(len(far))]
    return np.exp2(a.ravel()).repeat(32)


def f64(x):
    return np.asarray(x).astype(np.float64)


def striped(idx):
    return np.tile(idx.reshape(-1, 16).T, (8, 1)).astype(np.uint16)


def unstriped(offs):
    return offs[:16].T.reshape(-1).astype(np.int64)


E2M1 = np.array([0.0, 0.5, 1.0, 1.5, 2.0, 3.0, 4.0, 6.0, -0.0, -0.5, -1.0, -1.5, -2.0, -3.0, -4.0, -6.0])


def pack_weight(w, fmt):
    k, n = w.shape
    w = f64(np.asarray(w, np.float32).astype(ml_dtypes.bfloat16)).reshape(k // 32, 32, n)
    amax = np.abs(w).max(1)
    if fmt == "e4m3":
        byte = np.frexp(amax)[1] - 1 + 127 - 7
    else:
        mant, ex = np.frexp(amax / 6.0)
        byte = np.where(mant > 0.5, ex, ex - 1) + 127
    byte = np.clip(np.where(amax > 0, byte, 1), 1, 254)
    scaled = (w * np.exp2(127.0 - byte)[:, None, :]).reshape(k, n).astype(np.float32)
    by_word = np.ascontiguousarray(scaled.reshape(k // 512, 128, 4, n).transpose(0, 1, 3, 2))
    if fmt == "e4m3":
        words = by_word.astype(ml_dtypes.float8_e4m3fn).view(np.uint8)
    else:
        c = by_word.astype(ml_dtypes.float4_e2m1fn).view(np.uint8) & 0xF
        words = (c[..., 0::2] | (c[..., 1::2] << 4)).reshape(k // 512, 128, 2 * n)
    return np.ascontiguousarray(words), np.ascontiguousarray(byte.astype(np.uint8).reshape(k // 512, 16, n))


def unpack_weight(words, scales, fmt):
    g, _, n = scales.shape
    words = np.ascontiguousarray(words).reshape(g, 128, n, -1)
    if fmt == "e4m3":
        vals = words.view(ml_dtypes.float8_e4m3fn).astype(np.float64)
    else:
        nib = np.empty((g, 128, n, 4), np.uint8)
        nib[..., 0::2] = words & 0xF
        nib[..., 1::2] = words >> 4
        vals = E2M1[nib]
    vals = vals * np.repeat(np.exp2(scales.astype(np.float64) - 127.0), 8, axis=1)[..., None]
    return vals.transpose(0, 1, 3, 2).reshape(g * 512, n)


K, T, E, C, N = 512, 640, 15, 128, 384
TOP = 3


def by_expert(wq, xq):
    return np.concatenate([wq[e].T @ xq[:, e * C:(e + 1) * C] for e in range(E)], axis=1)


def setup_inputs():
    n = np.random.standard_normal
    s = mx_kscale(K)[:, None]
    deal = np.repeat(np.arange(E), C).reshape(TOP, T)[:, np.random.permutation(T)]
    deal = np.take_along_axis(deal, np.argsort(np.random.rand(TOP, T), axis=0), axis=0)
    for _ in range(8):
        s_, t_ = np.random.permutation(T).reshape(2, -1); r = np.random.randint(TOP, size=T // 2); x, y = deal[r, s_].copy(), deal[r, t_].copy()
        ok = ~((deal[:, s_] == y).any(0) | (deal[:, t_] == x).any(0)); deal[r[ok], s_[ok]] = y[ok]; deal[r[ok], t_[ok]] = x[ok]
    order = np.lexsort((np.random.rand(TOP * T), deal.reshape(-1)))
    slot_token = order % T; pos = np.empty(TOP * T, np.int64); pos[order] = np.arange(TOP * T); pos = pos.reshape(TOP, T)
    g = np.random.uniform(0.5, 1.5, (TOP, T)); g = g / g.sum(0)
    x = pack_weight(n((K, T)) * s, "e4m3")
    return {
        "x_words": x[0],
        "x_scales": x[1],
        "w": (n((E + 1, K, N)) / np.sqrt(K) / s[None]).astype(np.float32),
        "gate": np.stack([np.tile(r, (N, 1)) for r in g]).astype(np.float32),
        "offs": striped(slot_token),
        "pos1": striped(pos[0]),
        "pos2": striped(pos[1]),
        "pos3": striped(pos[2]),
    }


def reference(x_words, x_scales, w, gate, offs, pos1, pos2, pos3):
    idx = unstriped(offs)
    wq = mxq(f64(w), 1, "e4m3")
    xs = unpack_weight(x_words, x_scales, "e4m3")
    ys = wq[E].T @ xs
    xq = unpack_weight(x_words, x_scales, "e4m3")[:, idx]
    y = by_expert(wq, xq)
    return ys + sum(f64(gate[r]) * y[:, unstriped(p)] for r, p in enumerate((pos1, pos2, pos3)))

@@ -1,0 +1,189 @@
+from contextlib import ExitStack
+
+import concourse.mybir as mybir
+
+K, T, E, C, N = 512, 640, 15, 128, 384
+TOP = 3
+SLOTS = E * C
+FLOPS = 2 * K * N * (SLOTS + T)
+BYTES = (E + 1) * K * N * 4 + K * T + 16 * T + TOP * T * 4 + N * T * 4
+
+F32 = mybir.dt.float32
+BF16 = mybir.dt.bfloat16
+I32 = mybir.dt.int32
+U32 = mybir.dt.uint32
+U16 = mybir.dt.uint16
+U8 = mybir.dt.uint8
+FP8X4 = mybir.dt.float8_e4m3fn_x4
+MULT = mybir.AluOpType.mult
+ADD = mybir.AluOpType.add
+
+P = 128
+PACK = 4
+BLOCKS = N // P
+MATRICES = E + 1
+GROUP = 4
+BANK = 512
+WINDOW = 704
+PIECES = ((0, 384), (384, 640))
+LAG = 6
+VECTOR_CASTS = {(1, 10), (1, 11), (1, 14), (2, 7), (2, 10), (2, 11), (2, 12), (2, 14)}
+REGION = GROUP * P * PACK * 2
+
+
+def tile_moe_shr_lin_none_kernel(tc, x_words, x_scales, w, gate, offs, pos1, pos2, pos3, out):
+    nc = tc.nc
+    with ExitStack() as ctx:
+        lists = ctx.enter_context(tc.tile_pool(name="lists", bufs=1))
+        keep = ctx.enter_context(tc.tile_pool(name="keep", bufs=1))
+        shared = ctx.enter_context(tc.tile_pool(name="shared", bufs=1))
+        stage = ctx.enter_context(tc.tile_pool(name="stage", bufs=4))
+        routed_psum = ctx.enter_context(tc.psum_pool(name="routed_psum", bufs=4))
+        shared_psum = ctx.enter_context(tc.psum_pool(name="shared_psum", bufs=2))
+
+        steps = []
+        for b in range(BLOCKS):
+            cuts = (0, 4, 8, 12, 16) if b < BLOCKS - 1 else (0, 4, 8, 12, 14, 15, 16)
+            steps.extend((b, e0, e1) for e0, e1 in zip(cuts, cuts[1:]))
+
+        offs_sb = lists.tile([P, SLOTS // 16], U16, name="offs_sb")
+        pos_sb = [lists.tile([P, T // 16], U16, name=f"pos_sb{r}") for r in range(TOP)]
+        words = keep.tile([P, WINDOW], I32, name="words", align_bytes=64)
+        scales = keep.tile([P, WINDOW], U8, name="scales", align_bytes=64)
+        gates = keep.tile([P, TOP, T], F32, name="gates")
+        y = [keep.tile([P, SLOTS], F32, name=f"y{b}") for b in range(BLOCKS)]
+
+        raw = {}
+        for b in range(BLOCKS):
+            for g in range(3):
+                later = divmod(b * MATRICES + g * GROUP + GROUP - 1 + LAG, MATRICES)
+                if later < (BLOCKS - 1, E - 1):
+                    raw[later] = y[b][:, g * BANK:(g + 1) * BANK]
+        for b in range(BLOCKS):
+            for e in range(MATRICES):
+                if (b, e) not in raw:
+                    own = keep.tile([P, PACK * P], F32, name=f"raw{b}_{e}")
+                    raw[b, e] = own[:]
+
+        def load_w(b, e):
+            nc.sync.dma_start(out=raw[b, e].rearrange("p (j n) -> p j n", j=PACK),
+                              in_=w[e, :, b * P:(b + 1) * P].rearrange("(p j) n -> p j n", j=PACK))
+
+        nc.vector.memset(scales[:].bitcast(I32), 0)
+        nc.vector.memset(words[:, T:WINDOW], 0)
+        nc.sync.dma_start(out=words[:, 0:T], in_=x_words[0].rearrange("p t r -> p (t r)").bitcast(I32))
+        nc.sync.dma_start(offs_sb[:], offs)
+        for r in range(4):
+            nc.sync.dma_start(out=scales[r:P:32, 0:T].bitcast(I32), in_=x_scales[0, r:16:4, :].bitcast(I32))
+        for e in range(MATRICES):
+            load_w(0, e)
+            if 8 <= e < 8 + TOP:
+                nc.sync.dma_start(pos_sb[e - 8][:], (pos1, pos2, pos3)[e - 8])
+        nc.sync.dma_start(out=gates[:], in_=gate[:, 0:P, :].rearrange("r p t -> p r t"))
+        for b in range(1, BLOCKS):
+            for e in range(MATRICES):
+                load_w(b, e)
+
+        slot_words, slot_scales = {}, {}
+
+        def gather_tokens(g):
+            s0, s1 = g * BANK, min((g + 1) * BANK, SLOTS)
+            if g == 0:
+                slot_words[g] = keep.tile([P, s1 - s0], U32, name="slot_words0", align_bytes=64)
+                slot_scales[g] = keep.tile([P, s1 - s0], U8, name="slot_scales0", align_bytes=64)
+            else:
+                at = (g - 1) * REGION
+                slot_words[g] = shared.tile([P, s1 - s0], U32, name=f"slot_words{g}", align_bytes=64, offset=at)
+                slot_scales[g] = shared.tile([P, s1 - s0], U8, name=f"slot_scales{g}", align_bytes=64, offset=at + 4 * BANK)
+            idx = offs_sb[:, s0 // 16:s1 // 16]
+            nc.vector.tensor_copy(slot_words[g][:], words[:].bitcast(U32).indirect(idx))
+            nc.vector.tensor_copy(slot_scales[g][:], scales[:].indirect(idx))
+
+        grouped, banks, ys = {}, {}, {}
+
+        def cast(n):
+            b, e0, e1 = steps[n]
+            grouped[n] = shared.tile([P, e1 - e0, P, PACK], BF16, name=f"grouped{n}", align_bytes=64, offset=n * REGION)
+            for e in range(e0, e1):
+                dst = grouped[n][:, e - e0].rearrange("p (c i) j -> p c j i", i=4)
+                src = raw[b, e].rearrange("p (j c i) -> p c j i", j=PACK, i=4)
+                if (b, e) in VECTOR_CASTS:
+                    nc.vector.tensor_copy(out=dst, in_=src)
+                else:
+                    nc.scalar.copy(out=dst, in_=src)
+
+        def multiply(n):
+            b, e0, e1 = steps[n]
+            width = (e1 - e0) * P
+            codes = stage.tile([P, GROUP * P], U32, name="codes", align_bytes=64)
+            w_scales = stage.tile([P, GROUP * P], U8, name="w_scales", align_bytes=64)
+            nc.vector.quantize_mx(out=codes[:, 0:width].bitcast(FP8X4), scales=w_scales[:, 0:width],
+                                  in_=grouped[n][:].rearrange("p e n j -> p (e n j)"))
+            if e0 < E:
+                banks[n] = routed_psum.tile([P, BANK], F32, name="routed")
+            for e in range(e0, e1):
+                cols = slice((e - e0) * P, (e - e0 + 1) * P)
+                if e < E:
+                    g, at = divmod(e * C, BANK)
+                    nc.tensor.matmul_mx(out=banks[n][:, cols], lhsT=codes[:, cols].bitcast(FP8X4), lhsT_scale=w_scales[:, cols],
+                                        rhs=slot_words[g][:, at:at + C].bitcast(FP8X4), rhs_scale=slot_scales[g][:, at:at + C],
+                                        start=True, stop=True)
+                else:
+                    for h, (t0, t1) in enumerate(PIECES):
+                        ys[b, h] = shared_psum.tile([P, BANK], F32, name=f"shared{h}")
+                        for s0 in range(t0, t1, 256):
+                            s1 = min(s0 + 256, t1)
+                            nc.tensor.matmul_mx(out=ys[b, h][:, s0 - t0:s1 - t0], lhsT=codes[:, cols].bitcast(FP8X4), lhsT_scale=w_scales[:, cols],
+                                                rhs=words[:, s0:s1].bitcast(FP8X4), rhs_scale=scales[:, s0:s1],
+                                                start=True, stop=True)
+
+        def evacuate(n):
+            b, e0, e1 = steps[n]
+            s0, s1 = e0 * C, min(e1, E) * C
+            if s0 < s1:
+                nc.scalar.copy(out=y[b][:, s0:s1], in_=banks[n][:, 0:s1 - s0])
+
+        picked = {}
+
+        def pick(b, r):
+            if r > 0 and b < BLOCKS - 1:
+                picked[b, r] = shared.tile([P, T], F32, name=f"picked{b}_{r}", align_bytes=64, offset=(4 * (b + 1) + r - 1) * REGION)
+            else:
+                picked[b, r] = keep.tile([P, T], F32, name=f"picked{b}_{r}")
+            nc.vector.tensor_tensor(picked[b, r][:], y[b][:].indirect(pos_sb[r][:]), gates[:, r, :], MULT)
+
+        def add_shared(b):
+            for h, (t0, t1) in enumerate(PIECES):
+                nc.vector.tensor_tensor(picked[b, 0][:, t0:t1], ys[b, h][:, 0:t1 - t0], picked[b, 0][:, t0:t1], ADD)
+
+        def add_picked(b, r):
+            for t0, t1 in PIECES:
+                nc.vector.tensor_tensor(picked[b, 0][:, t0:t1], picked[b, 0][:, t0:t1], picked[b, r][:, t0:t1], ADD)
+
+        def store(b):
+            for t0, t1 in PIECES:
+                nc.sync.dma_start(out=out[b * P:(b + 1) * P, t0:t1], in_=picked[b, 0][:, t0:t1])
+
+        def combine(b, part):
+            pick(b, part)
+            if part == 1:
+                add_shared(b)
+            if part == 2:
+                add_picked(b, 1)
+                add_picked(b, 2)
+                store(b)
+
+        last = {b: max(n for n, s in enumerate(steps) if s[0] == b) for b in range(BLOCKS)}
+        gather_tokens(0)
+        for n in range(len(steps) + 5):
+            if n < len(steps):
+                cast(n)
+            if 1 <= n <= len(steps):
+                multiply(n - 1)
+            if 1 <= n <= 3:
+                gather_tokens(n)
+            if 2 <= n < len(steps) + 2:
+                evacuate(n - 2)
+            for b in range(BLOCKS):
+                if 0 <= n - last[b] - 2 < TOP:
+                    combine(b, n - last[b] - 2)

@@ -1,6 +1,7 @@
 from contextlib import ExitStack
 
 import concourse.mybir as mybir
+from concourse.masks import make_identity
 
 K, T, E, C, N = 512, 640, 15, 128, 384
 TOP = 3
@@ -21,13 +22,14 @@ ADD = mybir.AluOpType.add
 P = 128
 PACK = 4
 BLOCKS = N // P
+LAST = BLOCKS - 1
 MATRICES = E + 1
 GROUP = 4
+WHOLE = 12
 BANK = 512
 WINDOW = 704
 PIECES = ((0, 384), (384, 640))
-LAG = 6
-VECTOR_CASTS = {(1, 10), (1, 11), (1, 14), (2, 7), (2, 10), (2, 11), (2, 12), (2, 14)}
+LATE_CUTS = ((12, 14), (14, 15), (15, 16))
 REGION = GROUP * P * PACK * 2
 
 
@@ -39,151 +41,178 @@ def tile_moe_shr_lin_none_kernel(tc, x_words, x_scales, w, gate, offs, pos1, pos
         shared = ctx.enter_context(tc.tile_pool(name="shared", bufs=1))
         stage = ctx.enter_context(tc.tile_pool(name="stage", bufs=4))
         routed_psum = ctx.enter_context(tc.psum_pool(name="routed_psum", bufs=4))
-        shared_psum = ctx.enter_context(tc.psum_pool(name="shared_psum", bufs=2))
+        token_psum = ctx.enter_context(tc.psum_pool(name="token_psum", bufs=1))
 
-        steps = []
-        for b in range(BLOCKS):
-            cuts = (0, 4, 8, 12, 16) if b < BLOCKS - 1 else (0, 4, 8, 12, 14, 15, 16)
-            steps.extend((b, e0, e1) for e0, e1 in zip(cuts, cuts[1:]))
+        region = {(0, 0): 0, (1, 0): 1, (2, 0): 2, (0, 4): 3, (1, 4): 1, (2, 4): 0, (0, 8): 4, (1, 8): 1, (2, 8): 3}
+        slot_region = {2: 2, 3: 0}
+        late_region = 5
+        turned_region = 7
+
+        def region_tile(shape, dtype, name, number, at=0):
+            return shared.tile(shape, dtype, name=name, align_bytes=64, offset=number * REGION + at)
 
         offs_sb = lists.tile([P, SLOTS // 16], U16, name="offs_sb")
         pos_sb = [lists.tile([P, T // 16], U16, name=f"pos_sb{r}") for r in range(TOP)]
         words = keep.tile([P, WINDOW], I32, name="words", align_bytes=64)
         scales = keep.tile([P, WINDOW], U8, name="scales", align_bytes=64)
-        gates = keep.tile([P, TOP, T], F32, name="gates")
+        gates = [keep.tile([P, T], F32, name=f"gate{r}") for r in range(TOP)]
         y = [keep.tile([P, SLOTS], F32, name=f"y{b}") for b in range(BLOCKS)]
+        identity = keep.tile([P, P], F32, name="identity")
+        make_identity(nc, identity[:])
 
-        raw = {}
+        whole = [keep.tile([P, PACK, N], F32, name=f"whole{e}") for e in range(WHOLE)]
+        raw = {(b, e): whole[e][:, :, b * P:(b + 1) * P] for e in range(WHOLE) for b in range(BLOCKS)}
+        for b, key in ((1, (0, 15)), (2, (1, 12))):
+            raw[key] = y[b][:, 2 * BANK:3 * BANK].rearrange("p (j n) -> p j n", j=PACK)
+        raw[LAST, 14] = region_tile([P, PACK, P], F32, "raw_last", turned_region)[:]
         for b in range(BLOCKS):
-            for g in range(3):
-                later = divmod(b * MATRICES + g * GROUP + GROUP - 1 + LAG, MATRICES)
-                if later < (BLOCKS - 1, E - 1):
-                    raw[later] = y[b][:, g * BANK:(g + 1) * BANK]
-        for b in range(BLOCKS):
-            for e in range(MATRICES):
+            for e in range(WHOLE, MATRICES):
                 if (b, e) not in raw:
-                    own = keep.tile([P, PACK * P], F32, name=f"raw{b}_{e}")
+                    own = keep.tile([P, PACK, P], F32, name=f"raw{b}_{e}")
                     raw[b, e] = own[:]
-
-        def load_w(b, e):
-            nc.sync.dma_start(out=raw[b, e].rearrange("p (j n) -> p j n", j=PACK),
-                              in_=w[e, :, b * P:(b + 1) * P].rearrange("(p j) n -> p j n", j=PACK))
 
         nc.vector.memset(scales[:].bitcast(I32), 0)
         nc.vector.memset(words[:, T:WINDOW], 0)
-        nc.sync.dma_start(out=words[:, 0:T], in_=x_words[0].rearrange("p t r -> p (t r)").bitcast(I32))
         nc.sync.dma_start(offs_sb[:], offs)
+        nc.sync.dma_start(out=words[:, 0:T], in_=x_words[0].rearrange("p t r -> p (t r)").bitcast(I32))
         for r in range(4):
             nc.sync.dma_start(out=scales[r:P:32, 0:T].bitcast(I32), in_=x_scales[0, r:16:4, :].bitcast(I32))
-        for e in range(MATRICES):
-            load_w(0, e)
-            if 8 <= e < 8 + TOP:
-                nc.sync.dma_start(pos_sb[e - 8][:], (pos1, pos2, pos3)[e - 8])
-        nc.sync.dma_start(out=gates[:], in_=gate[:, 0:P, :].rearrange("r p t -> p r t"))
-        for b in range(1, BLOCKS):
-            for e in range(MATRICES):
-                load_w(b, e)
+        for e in range(WHOLE):
+            nc.sync.dma_start(out=whole[e][:], in_=w[e].rearrange("(p j) n -> p j n", j=PACK))
+            if e >= WHOLE - TOP:
+                nc.sync.dma_start(pos_sb[e - WHOLE + TOP][:], (pos1, pos2, pos3)[e - WHOLE + TOP])
+        gate_after = {(0, 15): 0, (1, 12): 1, (1, 15): 2}
+        for b in range(BLOCKS):
+            for e in range(WHOLE, MATRICES):
+                nc.sync.dma_start(out=raw[b, e], in_=w[e, :, b * P:(b + 1) * P].rearrange("(p j) n -> p j n", j=PACK))
+                if (b, e) in gate_after:
+                    nc.sync.dma_start(out=gates[gate_after[b, e]][:], in_=gate[gate_after[b, e], 0:P, :])
 
         slot_words, slot_scales = {}, {}
 
         def gather_tokens(g):
             s0, s1 = g * BANK, min((g + 1) * BANK, SLOTS)
-            if g == 0:
-                slot_words[g] = keep.tile([P, s1 - s0], U32, name="slot_words0", align_bytes=64)
-                slot_scales[g] = keep.tile([P, s1 - s0], U8, name="slot_scales0", align_bytes=64)
+            if g in slot_region:
+                slot_words[g] = region_tile([P, s1 - s0], U32, f"slot_words{g}", slot_region[g])
+                slot_scales[g] = region_tile([P, s1 - s0], U8, f"slot_scales{g}", slot_region[g], 4 * BANK)
             else:
-                at = (g - 1) * REGION
-                slot_words[g] = shared.tile([P, s1 - s0], U32, name=f"slot_words{g}", align_bytes=64, offset=at)
-                slot_scales[g] = shared.tile([P, s1 - s0], U8, name=f"slot_scales{g}", align_bytes=64, offset=at + 4 * BANK)
+                slot_words[g] = keep.tile([P, s1 - s0], U32, name=f"slot_words{g}", align_bytes=64)
+                slot_scales[g] = keep.tile([P, s1 - s0], U8, name=f"slot_scales{g}", align_bytes=64)
             idx = offs_sb[:, s0 // 16:s1 // 16]
             nc.vector.tensor_copy(slot_words[g][:], words[:].bitcast(U32).indirect(idx))
             nc.vector.tensor_copy(slot_scales[g][:], scales[:].indirect(idx))
 
-        grouped, banks, ys = {}, {}, {}
+        grouped, banks, ys, ys_sb, picked = {}, {}, {}, {}, {}
 
-        def cast(n):
-            b, e0, e1 = steps[n]
-            grouped[n] = shared.tile([P, e1 - e0, P, PACK], BF16, name=f"grouped{n}", align_bytes=64, offset=n * REGION)
-            for e in range(e0, e1):
-                dst = grouped[n][:, e - e0].rearrange("p (c i) j -> p c j i", i=4)
-                src = raw[b, e].rearrange("p (j c i) -> p c j i", j=PACK, i=4)
-                if (b, e) in VECTOR_CASTS:
-                    nc.vector.tensor_copy(out=dst, in_=src)
-                else:
-                    nc.scalar.copy(out=dst, in_=src)
+        def cast(b, e):
+            g, i = divmod(e, GROUP)
+            if i == 0 and e < WHOLE:
+                grouped[b, g] = region_tile([P, GROUP, P, PACK], BF16, f"grouped{b}_{g}", region[b, e])
+            elif i == 0:
+                grouped[b, g] = region_tile([P, GROUP, P, PACK], BF16, f"grouped{b}_{g}", late_region, (LAST - b) * 1024)
+            dst = grouped[b, g][:, i].rearrange("p (c i) j -> p c j i", i=4)
+            src = raw[b, e].rearrange("p j (c i) -> p c j i", i=4)
+            if e < WHOLE and (b == 2 or (b == 1 and e % 2 == 1)):
+                nc.vector.tensor_copy(out=dst, in_=src)
+            else:
+                nc.scalar.copy(out=dst, in_=src)
 
-        def multiply(n):
-            b, e0, e1 = steps[n]
+        def multiply(b, e0, e1):
             width = (e1 - e0) * P
             codes = stage.tile([P, GROUP * P], U32, name="codes", align_bytes=64)
             w_scales = stage.tile([P, GROUP * P], U8, name="w_scales", align_bytes=64)
             nc.vector.quantize_mx(out=codes[:, 0:width].bitcast(FP8X4), scales=w_scales[:, 0:width],
-                                  in_=grouped[n][:].rearrange("p e n j -> p (e n j)"))
-            if e0 < E:
-                banks[n] = routed_psum.tile([P, BANK], F32, name="routed")
+                                  in_=grouped[b, e0 // GROUP][:, e0 % GROUP:e0 % GROUP + e1 - e0].rearrange("p e n j -> p (e n j)"))
             for e in range(e0, e1):
                 cols = slice((e - e0) * P, (e - e0 + 1) * P)
                 if e < E:
                     g, at = divmod(e * C, BANK)
-                    nc.tensor.matmul_mx(out=banks[n][:, cols], lhsT=codes[:, cols].bitcast(FP8X4), lhsT_scale=w_scales[:, cols],
+                    if at == 0:
+                        banks[b, g] = routed_psum.tile([P, BANK], F32, name="routed")
+                    nc.tensor.matmul_mx(out=banks[b, g][:, at:at + C], lhsT=codes[:, cols].bitcast(FP8X4), lhsT_scale=w_scales[:, cols],
                                         rhs=slot_words[g][:, at:at + C].bitcast(FP8X4), rhs_scale=slot_scales[g][:, at:at + C],
                                         start=True, stop=True)
                 else:
                     for h, (t0, t1) in enumerate(PIECES):
-                        ys[b, h] = shared_psum.tile([P, BANK], F32, name=f"shared{h}")
+                        ys[b, h] = token_psum.tile([P, BANK], F32, name=f"shared{h}")
                         for s0 in range(t0, t1, 256):
                             s1 = min(s0 + 256, t1)
                             nc.tensor.matmul_mx(out=ys[b, h][:, s0 - t0:s1 - t0], lhsT=codes[:, cols].bitcast(FP8X4), lhsT_scale=w_scales[:, cols],
                                                 rhs=words[:, s0:s1].bitcast(FP8X4), rhs_scale=scales[:, s0:s1],
                                                 start=True, stop=True)
 
-        def evacuate(n):
-            b, e0, e1 = steps[n]
-            s0, s1 = e0 * C, min(e1, E) * C
-            if s0 < s1:
-                nc.scalar.copy(out=y[b][:, s0:s1], in_=banks[n][:, 0:s1 - s0])
+        def evacuate(b, g):
+            s0, s1 = g * BANK, min((g + 1) * BANK, SLOTS)
+            nc.scalar.copy(out=y[b][:, s0:s1], in_=banks[b, g][:, 0:s1 - s0])
 
-        picked = {}
+        def evacuate_shared(b):
+            ys_sb[b] = keep.tile([P, T], F32, name=f"ys_sb{b}")
+            for h, (t0, t1) in enumerate(PIECES):
+                nc.scalar.copy(out=ys_sb[b][:, t0:t1], in_=ys[b, h][:, 0:t1 - t0])
 
         def pick(b, r):
-            if r > 0 and b < BLOCKS - 1:
-                picked[b, r] = shared.tile([P, T], F32, name=f"picked{b}_{r}", align_bytes=64, offset=(4 * (b + 1) + r - 1) * REGION)
+            if b < LAST and r == TOP - 1:
+                picked[b, r] = region_tile([P, T], F32, f"picked{b}_{r}", late_region, REGION if b == 0 else 0)
             else:
                 picked[b, r] = keep.tile([P, T], F32, name=f"picked{b}_{r}")
-            nc.vector.tensor_tensor(picked[b, r][:], y[b][:].indirect(pos_sb[r][:]), gates[:, r, :], MULT)
+            nc.vector.tensor_tensor(picked[b, r][:], y[b][:].indirect(pos_sb[r][:]), gates[r][:], MULT)
 
-        def add_shared(b):
+        def turn_and_add(terms, result):
             for h, (t0, t1) in enumerate(PIECES):
-                nc.vector.tensor_tensor(picked[b, 0][:, t0:t1], ys[b, h][:, 0:t1 - t0], picked[b, 0][:, t0:t1], ADD)
+                bank = token_psum.tile([P, BANK], F32, name=f"turned{h}")
+                for at in range(t0, t1, P):
+                    for n, term in enumerate(terms):
+                        nc.tensor.matmul(bank[:, at - t0:at - t0 + P], term[:, at:at + P], identity[:],
+                                         start=(n == 0), stop=(n == len(terms) - 1), is_transpose=True)
+                nc.scalar.copy(out=result[:, t0:t1], in_=bank[:, 0:t1 - t0])
 
-        def add_picked(b, r):
-            for t0, t1 in PIECES:
-                nc.vector.tensor_tensor(picked[b, 0][:, t0:t1], picked[b, 0][:, t0:t1], picked[b, r][:, t0:t1], ADD)
+        def sum_on_tensor(b):
+            turned = region_tile([P, T], F32, f"turned_sb{b}", turned_region)
+            turn_and_add([ys_sb[b]] + [picked[b, r] for r in range(TOP)], turned)
+            total = keep.tile([P, T], F32, name=f"total{b}")
+            turn_and_add([turned], total)
+            nc.sync.dma_start(out=out[b * P:(b + 1) * P, :], in_=total[:])
 
-        def store(b):
-            for t0, t1 in PIECES:
-                nc.sync.dma_start(out=out[b * P:(b + 1) * P, t0:t1], in_=picked[b, 0][:, t0:t1])
+        def late_groups(b):
+            for e0, e1 in LATE_CUTS:
+                for e in range(e0, e1):
+                    cast(b, e)
+                multiply(b, e0, e1)
 
-        def combine(b, part):
-            pick(b, part)
-            if part == 1:
-                add_shared(b)
-            if part == 2:
-                add_picked(b, 1)
-                add_picked(b, 2)
-                store(b)
-
-        last = {b: max(n for n, s in enumerate(steps) if s[0] == b) for b in range(BLOCKS)}
         gather_tokens(0)
-        for n in range(len(steps) + 5):
-            if n < len(steps):
-                cast(n)
-            if 1 <= n <= len(steps):
-                multiply(n - 1)
-            if 1 <= n <= 3:
-                gather_tokens(n)
-            if 2 <= n < len(steps) + 2:
-                evacuate(n - 2)
+        gather_tokens(1)
+        for g in range(WHOLE // GROUP):
+            e0, e1 = g * GROUP, (g + 1) * GROUP
+            for e in range(e0, e1):
+                for b in range(BLOCKS):
+                    cast(b, e)
             for b in range(BLOCKS):
-                if 0 <= n - last[b] - 2 < TOP:
-                    combine(b, n - last[b] - 2)
+                multiply(b, e0, e1)
+            if g < 2:
+                gather_tokens(g + 2)
+            for b in range(BLOCKS if g < 2 else 1):
+                evacuate(b, g)
+
+        for b in range(BLOCKS):
+            late_groups(b)
+            evacuate(b, 3)
+            if b < LAST:
+                evacuate(b + 1, 2)
+                evacuate_shared(b)
+            if b > 0:
+                pick(b - 1, 2)
+                if b > 1:
+                    sum_on_tensor(b - 2)
+            pick(b, 0)
+            pick(b, 1)
+        sum_on_tensor(LAST - 1)
+
+        total = picked[LAST, 0]
+        for h, (t0, t1) in enumerate(PIECES):
+            nc.vector.tensor_tensor(total[:, t0:t1], ys[LAST, h][:, 0:t1 - t0], total[:, t0:t1], ADD)
+        pick(LAST, 2)
+        for t0, t1 in PIECES:
+            nc.vector.tensor_tensor(total[:, t0:t1], total[:, t0:t1], picked[LAST, 1][:, t0:t1], ADD)
+        for t0, t1 in PIECES:
+            nc.vector.tensor_tensor(total[:, t0:t1], total[:, t0:t1], picked[LAST, 2][:, t0:t1], ADD)
+            nc.sync.dma_start(out=out[LAST * P:(LAST + 1) * P, t0:t1], in_=total[:, t0:t1])

from contextlib import ExitStack

import concourse.mybir as mybir
from concourse.masks import make_identity

K, T, E, C, N = 512, 640, 15, 128, 384
TOP = 3
SLOTS = E * C
FLOPS = 2 * K * N * (SLOTS + T)
BYTES = (E + 1) * K * N * 4 + K * T + 16 * T + TOP * T * 4 + N * T * 4

F32 = mybir.dt.float32
BF16 = mybir.dt.bfloat16
I32 = mybir.dt.int32
U32 = mybir.dt.uint32
U16 = mybir.dt.uint16
U8 = mybir.dt.uint8
FP8X4 = mybir.dt.float8_e4m3fn_x4
MULT = mybir.AluOpType.mult
ADD = mybir.AluOpType.add

P = 128
PACK = 4
BLOCKS = N // P
LAST = BLOCKS - 1
MATRICES = E + 1
GROUP = 4
WHOLE = 12
BANK = 512
WINDOW = 704
PIECES = ((0, 384), (384, 640))
LATE_CUTS = ((12, 14), (14, 15), (15, 16))
REGION = GROUP * P * PACK * 2


def tile_moe_shr_lin_none_kernel(tc, x_words, x_scales, w, gate, offs, pos1, pos2, pos3, out):
    nc = tc.nc
    with ExitStack() as ctx:
        lists = ctx.enter_context(tc.tile_pool(name="lists", bufs=1))
        keep = ctx.enter_context(tc.tile_pool(name="keep", bufs=1))
        shared = ctx.enter_context(tc.tile_pool(name="shared", bufs=1))
        stage = ctx.enter_context(tc.tile_pool(name="stage", bufs=4))
        routed_psum = ctx.enter_context(tc.psum_pool(name="routed_psum", bufs=4))
        token_psum = ctx.enter_context(tc.psum_pool(name="token_psum", bufs=1))

        region = {(0, 0): 0, (1, 0): 1, (2, 0): 2, (0, 4): 3, (1, 4): 1, (2, 4): 0, (0, 8): 4, (1, 8): 1, (2, 8): 3}
        slot_region = {2: 2, 3: 0}
        late_region = 5
        turned_region = 7

        def region_tile(shape, dtype, name, number, at=0):
            return shared.tile(shape, dtype, name=name, align_bytes=64, offset=number * REGION + at)

        offs_sb = lists.tile([P, SLOTS // 16], U16, name="offs_sb")
        pos_sb = [lists.tile([P, T // 16], U16, name=f"pos_sb{r}") for r in range(TOP)]
        words = keep.tile([P, WINDOW], I32, name="words", align_bytes=64)
        scales = keep.tile([P, WINDOW], U8, name="scales", align_bytes=64)
        gates = [keep.tile([P, T], F32, name=f"gate{r}") for r in range(TOP)]
        y = [keep.tile([P, SLOTS], F32, name=f"y{b}") for b in range(BLOCKS)]
        identity = keep.tile([P, P], F32, name="identity")
        make_identity(nc, identity[:])

        whole = [keep.tile([P, PACK, N], F32, name=f"whole{e}") for e in range(WHOLE)]
        raw = {(b, e): whole[e][:, :, b * P:(b + 1) * P] for e in range(WHOLE) for b in range(BLOCKS)}
        for b, key in ((1, (0, 15)), (2, (1, 12))):
            raw[key] = y[b][:, 2 * BANK:3 * BANK].rearrange("p (j n) -> p j n", j=PACK)
        raw[LAST, 14] = region_tile([P, PACK, P], F32, "raw_last", turned_region)[:]
        for b in range(BLOCKS):
            for e in range(WHOLE, MATRICES):
                if (b, e) not in raw:
                    own = keep.tile([P, PACK, P], F32, name=f"raw{b}_{e}")
                    raw[b, e] = own[:]

        nc.vector.memset(scales[:].bitcast(I32), 0)
        nc.vector.memset(words[:, T:WINDOW], 0)
        nc.sync.dma_start(offs_sb[:], offs)
        nc.sync.dma_start(out=words[:, 0:T], in_=x_words[0].rearrange("p t r -> p (t r)").bitcast(I32))
        for r in range(4):
            nc.sync.dma_start(out=scales[r:P:32, 0:T].bitcast(I32), in_=x_scales[0, r:16:4, :].bitcast(I32))
        for e in range(WHOLE):
            nc.sync.dma_start(out=whole[e][:], in_=w[e].rearrange("(p j) n -> p j n", j=PACK))
            if e >= WHOLE - TOP:
                nc.sync.dma_start(pos_sb[e - WHOLE + TOP][:], (pos1, pos2, pos3)[e - WHOLE + TOP])
        gate_after = {(0, 15): 0, (1, 12): 1, (1, 15): 2}
        for b in range(BLOCKS):
            for e in range(WHOLE, MATRICES):
                nc.sync.dma_start(out=raw[b, e], in_=w[e, :, b * P:(b + 1) * P].rearrange("(p j) n -> p j n", j=PACK))
                if (b, e) in gate_after:
                    nc.sync.dma_start(out=gates[gate_after[b, e]][:], in_=gate[gate_after[b, e], 0:P, :])

        slot_words, slot_scales = {}, {}

        def gather_tokens(g):
            s0, s1 = g * BANK, min((g + 1) * BANK, SLOTS)
            if g in slot_region:
                slot_words[g] = region_tile([P, s1 - s0], U32, f"slot_words{g}", slot_region[g])
                slot_scales[g] = region_tile([P, s1 - s0], U8, f"slot_scales{g}", slot_region[g], 4 * BANK)
            else:
                slot_words[g] = keep.tile([P, s1 - s0], U32, name=f"slot_words{g}", align_bytes=64)
                slot_scales[g] = keep.tile([P, s1 - s0], U8, name=f"slot_scales{g}", align_bytes=64)
            idx = offs_sb[:, s0 // 16:s1 // 16]
            nc.vector.tensor_copy(slot_words[g][:], words[:].bitcast(U32).indirect(idx))
            nc.vector.tensor_copy(slot_scales[g][:], scales[:].indirect(idx))

        grouped, banks, ys, ys_sb, picked = {}, {}, {}, {}, {}

        def cast(b, e):
            g, i = divmod(e, GROUP)
            if i == 0 and e < WHOLE:
                grouped[b, g] = region_tile([P, GROUP, P, PACK], BF16, f"grouped{b}_{g}", region[b, e])
            elif i == 0:
                grouped[b, g] = region_tile([P, GROUP, P, PACK], BF16, f"grouped{b}_{g}", late_region, (LAST - b) * 1024)
            dst = grouped[b, g][:, i].rearrange("p (c i) j -> p c j i", i=4)
            src = raw[b, e].rearrange("p j (c i) -> p c j i", i=4)
            if e < WHOLE and (b == 2 or (b == 1 and e % 2 == 1)):
                nc.vector.tensor_copy(out=dst, in_=src)
            else:
                nc.scalar.copy(out=dst, in_=src)

        def multiply(b, e0, e1):
            width = (e1 - e0) * P
            codes = stage.tile([P, GROUP * P], U32, name="codes", align_bytes=64)
            w_scales = stage.tile([P, GROUP * P], U8, name="w_scales", align_bytes=64)
            nc.vector.quantize_mx(out=codes[:, 0:width].bitcast(FP8X4), scales=w_scales[:, 0:width],
                                  in_=grouped[b, e0 // GROUP][:, e0 % GROUP:e0 % GROUP + e1 - e0].rearrange("p e n j -> p (e n j)"))
            for e in range(e0, e1):
                cols = slice((e - e0) * P, (e - e0 + 1) * P)
                if e < E:
                    g, at = divmod(e * C, BANK)
                    if at == 0:
                        banks[b, g] = routed_psum.tile([P, BANK], F32, name="routed")
                    nc.tensor.matmul_mx(out=banks[b, g][:, at:at + C], lhsT=codes[:, cols].bitcast(FP8X4), lhsT_scale=w_scales[:, cols],
                                        rhs=slot_words[g][:, at:at + C].bitcast(FP8X4), rhs_scale=slot_scales[g][:, at:at + C],
                                        start=True, stop=True)
                else:
                    for h, (t0, t1) in enumerate(PIECES):
                        ys[b, h] = token_psum.tile([P, BANK], F32, name=f"shared{h}")
                        for s0 in range(t0, t1, 256):
                            s1 = min(s0 + 256, t1)
                            nc.tensor.matmul_mx(out=ys[b, h][:, s0 - t0:s1 - t0], lhsT=codes[:, cols].bitcast(FP8X4), lhsT_scale=w_scales[:, cols],
                                                rhs=words[:, s0:s1].bitcast(FP8X4), rhs_scale=scales[:, s0:s1],
                                                start=True, stop=True)

        def evacuate(b, g):
            s0, s1 = g * BANK, min((g + 1) * BANK, SLOTS)
            nc.scalar.copy(out=y[b][:, s0:s1], in_=banks[b, g][:, 0:s1 - s0])

        def evacuate_shared(b):
            ys_sb[b] = keep.tile([P, T], F32, name=f"ys_sb{b}")
            for h, (t0, t1) in enumerate(PIECES):
                nc.scalar.copy(out=ys_sb[b][:, t0:t1], in_=ys[b, h][:, 0:t1 - t0])

        def pick(b, r):
            if b < LAST and r == TOP - 1:
                picked[b, r] = region_tile([P, T], F32, f"picked{b}_{r}", late_region, REGION if b == 0 else 0)
            else:
                picked[b, r] = keep.tile([P, T], F32, name=f"picked{b}_{r}")
            nc.vector.tensor_tensor(picked[b, r][:], y[b][:].indirect(pos_sb[r][:]), gates[r][:], MULT)

        def turn_and_add(terms, result):
            for h, (t0, t1) in enumerate(PIECES):
                bank = token_psum.tile([P, BANK], F32, name=f"turned{h}")
                for at in range(t0, t1, P):
                    for n, term in enumerate(terms):
                        nc.tensor.matmul(bank[:, at - t0:at - t0 + P], term[:, at:at + P], identity[:],
                                         start=(n == 0), stop=(n == len(terms) - 1), is_transpose=True)
                nc.scalar.copy(out=result[:, t0:t1], in_=bank[:, 0:t1 - t0])

        def sum_on_tensor(b):
            turned = region_tile([P, T], F32, f"turned_sb{b}", turned_region)
            turn_and_add([ys_sb[b]] + [picked[b, r] for r in range(TOP)], turned)
            total = keep.tile([P, T], F32, name=f"total{b}")
            turn_and_add([turned], total)
            nc.sync.dma_start(out=out[b * P:(b + 1) * P, :], in_=total[:])

        def late_groups(b):
            for e0, e1 in LATE_CUTS:
                for e in range(e0, e1):
                    cast(b, e)
                multiply(b, e0, e1)

        gather_tokens(0)
        gather_tokens(1)
        for g in range(WHOLE // GROUP):
            e0, e1 = g * GROUP, (g + 1) * GROUP
            for e in range(e0, e1):
                for b in range(BLOCKS):
                    cast(b, e)
            for b in range(BLOCKS):
                multiply(b, e0, e1)
            if g < 2:
                gather_tokens(g + 2)
            for b in range(BLOCKS if g < 2 else 1):
                evacuate(b, g)

        for b in range(BLOCKS):
            late_groups(b)
            evacuate(b, 3)
            if b < LAST:
                evacuate(b + 1, 2)
                evacuate_shared(b)
            if b > 0:
                pick(b - 1, 2)
                if b > 1:
                    sum_on_tensor(b - 2)
            pick(b, 0)
            pick(b, 1)
        sum_on_tensor(LAST - 1)

        total = picked[LAST, 0]
        for h, (t0, t1) in enumerate(PIECES):
            nc.vector.tensor_tensor(total[:, t0:t1], ys[LAST, h][:, 0:t1 - t0], total[:, t0:t1], ADD)
        pick(LAST, 2)
        for t0, t1 in PIECES:
            nc.vector.tensor_tensor(total[:, t0:t1], total[:, t0:t1], picked[LAST, 1][:, t0:t1], ADD)
        for t0, t1 in PIECES:
            nc.vector.tensor_tensor(total[:, t0:t1], total[:, t0:t1], picked[LAST, 2][:, t0:t1], ADD)
            nc.sync.dma_start(out=out[LAST * P:(LAST + 1) * P, t0:t1], in_=total[:, t0:t1])
